import numpy as np, ml_dtypes
CORES = [3,5,19,21,35,37,51,53,67,69]
N = 10
QP = 32
def setup_inputs(rng):
    m = 150 * rng.standard_normal((1, QP, 1), dtype=np.float32) + 3 * rng.standard_normal((N, QP, 1), dtype=np.float32)
    m = (m + rng.uniform(100, 300, (1, QP, 1)) * (rng.random((1, QP, 1)) < 0.7) * (rng.random((N, QP, 1)) < 0.5)).astype(np.float32)
    l = 20 * (1 + np.abs(rng.standard_normal((N, QP, 1), dtype=np.float32)))
    return {"o": (l * rng.standard_normal((N, QP, 128), dtype=np.float32) / 4).astype(ml_dtypes.bfloat16), "ml": np.concatenate([m, l], axis=2)}
def setup_inputs_big(rng):
    d = setup_inputs(rng)
    for k in ("o",): d[k] = (d[k].astype(np.float32) * 1048576.0).astype(d[k].dtype)
    return d
def setup_inputs_small(rng):
    d = setup_inputs(rng)
    for k in ("o",): d[k] = (d[k].astype(np.float32) * (1 / 1048576.0)).astype(d[k].dtype)
    return d
def setup_inputs_apart(rng):
    d = setup_inputs(rng)
    f = (10.0 ** rng.permutation(np.linspace(-1.5, 1.5, N))).astype(np.float32).reshape(N, 1, 1)
    for k in ("o",): d[k] = (d[k].astype(np.float32) * f).astype(d[k].dtype)
    return d
def reference(o, ml):
    O, ML = o.astype(np.float64), ml.astype(np.float64)
    m, l = ML[:, :, 0:1], ML[:, :, 1:2]
    f = np.exp(m - m.max(axis=0))
    y = ((f * O).sum(axis=0) / (f * l).sum(axis=0)).astype(ml_dtypes.bfloat16)
    return {"y": np.broadcast_to(y, (N,) + y.shape)}

@@ -1,0 +1,138 @@
+from concourse.bass import DstId, RemoteDMATransfer
+from concourse.mybir import AluOpType, AxisListType, ActivationFunctionType
+
+N = 10
+K2 = 7
+INV = 1.0 / (2 ** K2)
+
+SCRATCH = {
+    "oland": ("dram", [N, 128, 32], "bfloat16"),
+    "mland": ("dram", [N, 128, 1], "float32"),
+    "X": ("sbuf", [128, 512], "bfloat16"),
+    "mlT": ("sbuf", [128, 64], "float32"),
+    "mlP": ("sbuf", [128, 8], "float32"),
+    "lb": ("sbuf", [128, 4], "bfloat16"),
+    "cinv": ("sbuf", [128, 80], "float32"),
+    "one1": ("sbuf", [128, 80], "float32"),
+    "Jsel": ("sbuf", [128, 80], "float32"),
+    "U": ("sbuf", [128, 80], "float32"),
+    "V": ("sbuf", [128, 32], "float32"),
+    "I32": ("sbuf", [128, 32], "float32"),
+    "negM": ("sbuf", [128, 4], "float32"),
+    "Dg": ("sbuf", [128, 32], "float32"),
+    "S": ("sbuf", [128, 32], "float32"),
+    "Wd": ("sbuf", [128, 32], "bfloat16"),
+    "rden": ("sbuf", [128, 4], "float32"),
+    "Y": ("sbuf", [128, 512], "bfloat16"),
+    "PT": ("psum", [128, 512], "float32"),
+    "PA": ("psum", [128, 512], "float32"),
+    "PD": ("psum", [128, 512], "float32"),
+    "PO1": ("psum", [128, 512], "float32"),
+    "PO2": ("psum", [128, 512], "float32"),
+}
+SEMAPHORES = ["ldm", "ldo", "mlarr", "oarr", "sent", "cst", "cg", "sT", "sP", "sX", "sT1", "sM", "sDg", "sL",
+              "sA", "sq", "sD", "sR", "sO1", "sO2", "fin", "st"]
+
+
+def rank_program(g, core, T, topo):
+    r = T.rank_of(core)
+    if r is None:
+        return
+    s = T.sem
+    others = [c for c in T.cores if c != core]
+    common = 0xFFFF
+    for c in others:
+        common &= topo.mask(core, c)
+    bits = [1 << b for b in range(16) if (common >> b) & 1]
+    ids = [DstId(rid=topo.addr(c)[0], pnc=topo.addr(c)[1]) for c in others]
+    e_ml = bits[0]
+    n_ml = 1
+    e_o = common
+    n_o = len(bits)
+
+    sy, ac, ve, pe = g.sync, g.scalar, g.vector, g.tensor
+    mT = T.mlT[0:10, 0:64:2]
+
+    sy.dma_start(T.mland[r, 0:64, :], T.ml[:, :]).then_inc(s.ldm, 16)
+    ac.dma_start(T.mland[r, 64:128, :], T.ml[:, :]).then_inc(s.ldm, 16)
+    sy.dma_start(T.oland[r], T.o[:, :]).then_inc(s.ldo, 16)
+
+    ve.memset(T.cinv[0:32, 0:80], INV).then_inc(s.cst, 1)
+    ve.memset(T.one1[0:32, 0:80], 1.0).then_inc(s.cst, 1)
+
+    g.wait_ge(s.ldm, 32)
+    g.remote_dma_fused([RemoteDMATransfer(dst_ids=ids, dma_engine_mask=e_ml, remote_sem=s.mlarr,
+                                          srcs=[T.mland[r]], dsts=[T.mland[r] for _ in others], alu_op=0)],
+                       local_sem=s.sent)
+    g.wait_ge(s.ldo, 16)
+    g.remote_dma_fused([RemoteDMATransfer(dst_ids=ids, dma_engine_mask=e_o, remote_sem=s.oarr,
+                                          srcs=[T.oland[r]], dsts=[T.oland[r] for _ in others], alu_op=0)],
+                       local_sem=s.sent)
+    g.wait_ge(s.cst, 2)
+    eq = AluOpType.is_equal
+    g.affine_select(T.U[0:8, 0:80], T.one1[0:8, 0:80], [[0, 10], [-1, 8]], eq, 0.0, 0, 1).then_inc(s.cg, 1)
+    g.affine_select(T.V[0:8, 0:32], T.one1[0:8, 0:32], [[-1, 8], [0, 4]], eq, 0.0, 0, 1).then_inc(s.cg, 1)
+    g.affine_select(T.I32[0:32, 0:32], T.one1[0:32, 0:32], [[-1, 32]], eq, 0.0, 0, 1).then_inc(s.cg, 1)
+    g.affine_select(T.Jsel[0:10, 0:80], T.cinv[0:10, 0:80], [[-1, 10], [0, 8]], eq, 0.0, 0, 1).then_inc(s.cg, 1)
+    g.wait_ge(s.sent, n_ml + n_o)
+
+    sy.wait_ge(s.ldm, 32)
+    sy.wait_ge(s.mlarr, 9 * n_ml)
+    sy.dma_start(T.mlT[0:10, 0:64], T.mland[:, 0:64, :]).then_inc(s.sT, 16)
+    sy.wait_ge(s.ldo, 16)
+    sy.wait_ge(s.oarr, 9 * n_o)
+    sy.dma_start(T.X[0:80, :], T.oland[:]).then_inc(s.sX, 16)
+
+    ac.wait_ge(s.ldm, 32)
+    ac.wait_ge(s.mlarr, 9 * n_ml)
+    ac.dma_start(T.mlP[0:80, 0:8], T.mland[:, 0:64, :]).then_inc(s.sP, 16)
+
+    pe.wait_ge(s.cg, 4)
+    pe.matmul(T.PA[0:80, 0:32], T.U[0:8, 0:80], T.V[0:8, 0:32], True, False)
+    pe.wait_ge(s.sT, 16)
+    pe.matmul(T.PT[0:32, 0:10], mT, T.I32[0:10, 0:10], True, True).then_inc(s.sT1, 1)
+    pe.matmul(T.PA[0:80, 0:32], T.Jsel[0:10, 0:80], mT, False, False)
+    pe.wait_ge(s.sDg, 1)
+    pe.matmul(T.PA[0:80, 0:32], T.cinv[0:32, 0:80], T.Dg[0:32, 0:32], False, True).then_inc(s.sA, 1)
+    pe.wait_ge(s.sq, K2 + 1)
+    pe.wait_ge(s.sL, 1)
+    for c in range(4):
+        pe.matmul(T.PD[0:8, c:c + 1], T.Wd[0:80, c:32:4], T.lb[0:80, c:c + 1], True, True).then_inc(s.sD, 1)
+    pe.wait_ge(s.sX, 16)
+    for c in range(4):
+        po, so = (T.PO1, s.sO1) if c < 2 else (T.PO2, s.sO2)
+        k = c % 2
+        pe.matmul(po[0:8, k * 128:(k + 1) * 128], T.Wd[0:80, c:32:4], T.X[0:80, c * 128:(c + 1) * 128],
+                  True, True).then_inc(so, 1)
+
+    ve.wait_ge(s.sT1, 1)
+    ve.tensor_reduce(T.negM[0:32, 0:1], T.PT[0:32, 0:10], AxisListType.X, AluOpType.max,
+                     negate=True).then_inc(s.sM, 1)
+    ve.wait_ge(s.sM, 1)
+    ve.wait_ge(s.cg, 4)
+    ve.tensor_scalar(T.Dg[0:32, 0:32], T.I32[0:32, 0:32], T.negM[0:32, 0:1], None, AluOpType.mult).then_inc(s.sDg, 1)
+    ve.wait_ge(s.sP, 16)
+    ve.tensor_copy(T.lb[0:80, 0:4], T.mlP[0:80, 1:8:2]).then_inc(s.sL, 1)
+    ve.wait_ge(s.sA, 1)
+    S = T.S[0:80, 0:32]
+    ve.tensor_scalar(S, T.PA[0:80, 0:32], 0.0, None, AluOpType.max).then_inc(s.sq, 1)
+    for i in range(K2):
+        ve.wait_ge(s.sq, i + 1)
+        out = S if i < K2 - 1 else T.Wd[0:80, 0:32]
+        ve.tensor_tensor(out, S, S, AluOpType.mult).then_inc(s.sq, 1)
+    ve.wait_ge(s.sD, 4)
+    ve.reciprocal(T.rden[0:8, 0:4], T.PD[0:8, 0:4]).then_inc(s.sR, 1)
+    ve.wait_ge(s.sR, 1)
+    ve.wait_ge(s.sO1, 2)
+    for c in (0, 1):
+        ve.tensor_scalar(T.Y[0:8, c * 128:(c + 1) * 128], T.PO1[0:8, c * 128:(c + 1) * 128],
+                         T.rden[0:8, c:c + 1], None, AluOpType.mult).then_inc(s.fin, 1)
+    ac.wait_ge(s.sR, 1)
+    ac.wait_ge(s.sO2, 2)
+    for c in (2, 3):
+        ac.activation(T.Y[0:8, c * 128:(c + 1) * 128], T.PO2[0:8, (c - 2) * 128:(c - 1) * 128],
+                      ActivationFunctionType.Copy, scale=T.rden[0:8, c:c + 1]).then_inc(s.fin, 1)
+
+    sy.wait_ge(s.fin, 4)
+    sy.dma_start(T.y[:, :], T.Y[0:8, :]).then_inc(s.st, 16)
+    sy.wait_ge(s.st, 16)

@@ -2,8 +2,9 @@ from concourse.bass import DstId, RemoteDMATransfer
 from concourse.mybir import AluOpType, AxisListType, ActivationFunctionType
 
 N = 10
-K2 = 7
+K2 = 4
 INV = 1.0 / (2 ** K2)
+NSTEP = K2 + 2
 
 SCRATCH = {
     "oland": ("dram", [N, 128, 32], "bfloat16"),
@@ -27,11 +28,13 @@ SCRATCH = {
     "PT": ("psum", [128, 512], "float32"),
     "PA": ("psum", [128, 512], "float32"),
     "PD": ("psum", [128, 512], "float32"),
+    "PO0": ("psum", [128, 512], "float32"),
     "PO1": ("psum", [128, 512], "float32"),
     "PO2": ("psum", [128, 512], "float32"),
+    "PO3": ("psum", [128, 512], "float32"),
 }
 SEMAPHORES = ["ldm", "ldo", "mlarr", "oarr", "sent", "cst", "cg", "sT", "sP", "sX", "sT1", "sM", "sDg", "sL",
-              "sA", "sq", "sD", "sR", "sO1", "sO2", "fin", "st"]
+              "sA", "sq", "sD", "sR", "sO0", "sO1", "sO2", "sO3", "fin", "st"]
 
 
 def rank_program(g, core, T, topo):
@@ -45,12 +48,11 @@ def rank_program(g, core, T, topo):
         common &= topo.mask(core, c)
     bits = [1 << b for b in range(16) if (common >> b) & 1]
     ids = [DstId(rid=topo.addr(c)[0], pnc=topo.addr(c)[1]) for c in others]
-    e_ml = bits[0]
-    n_ml = 1
-    e_o = common
-    n_o = len(bits)
+    e_ml, n_ml = bits[0], 1
+    e_o, n_o = common, len(bits)
 
     sy, ac, ve, pe = g.sync, g.scalar, g.vector, g.tensor
+    AF = ActivationFunctionType
     mT = T.mlT[0:10, 0:64:2]
 
     sy.dma_start(T.mland[r, 0:64, :], T.ml[:, :]).then_inc(s.ldm, 16)
@@ -87,6 +89,8 @@ def rank_program(g, core, T, topo):
     ac.wait_ge(s.mlarr, 9 * n_ml)
     ac.dma_start(T.mlP[0:80, 0:8], T.mland[:, 0:64, :]).then_inc(s.sP, 16)
 
+    PO = [T.PO0, T.PO1, T.PO2, T.PO3]
+    SO = [s.sO0, s.sO1, s.sO2, s.sO3]
     pe.wait_ge(s.cg, 4)
     pe.matmul(T.PA[0:80, 0:32], T.U[0:8, 0:80], T.V[0:8, 0:32], True, False)
     pe.wait_ge(s.sT, 16)
@@ -94,44 +98,47 @@ def rank_program(g, core, T, topo):
     pe.matmul(T.PA[0:80, 0:32], T.Jsel[0:10, 0:80], mT, False, False)
     pe.wait_ge(s.sDg, 1)
     pe.matmul(T.PA[0:80, 0:32], T.cinv[0:32, 0:80], T.Dg[0:32, 0:32], False, True).then_inc(s.sA, 1)
-    pe.wait_ge(s.sq, K2 + 1)
     pe.wait_ge(s.sL, 1)
+    pe.wait_ge(s.sq, NSTEP)
     for c in range(4):
         pe.matmul(T.PD[0:8, c:c + 1], T.Wd[0:80, c:32:4], T.lb[0:80, c:c + 1], True, True).then_inc(s.sD, 1)
     pe.wait_ge(s.sX, 16)
     for c in range(4):
-        po, so = (T.PO1, s.sO1) if c < 2 else (T.PO2, s.sO2)
-        k = c % 2
-        pe.matmul(po[0:8, k * 128:(k + 1) * 128], T.Wd[0:80, c:32:4], T.X[0:80, c * 128:(c + 1) * 128],
-                  True, True).then_inc(so, 1)
+        pe.matmul(PO[c][0:8, 0:128], T.Wd[0:80, c:32:4], T.X[0:80, c * 128:(c + 1) * 128],
+                  True, True).then_inc(SO[c], 1)
 
     ve.wait_ge(s.sT1, 1)
     ve.tensor_reduce(T.negM[0:32, 0:1], T.PT[0:32, 0:10], AxisListType.X, AluOpType.max,
                      negate=True).then_inc(s.sM, 1)
-    ve.wait_ge(s.sM, 1)
     ve.wait_ge(s.cg, 4)
+    ve.wait_ge(s.sM, 1)
     ve.tensor_scalar(T.Dg[0:32, 0:32], T.I32[0:32, 0:32], T.negM[0:32, 0:1], None, AluOpType.mult).then_inc(s.sDg, 1)
     ve.wait_ge(s.sP, 16)
     ve.tensor_copy(T.lb[0:80, 0:4], T.mlP[0:80, 1:8:2]).then_inc(s.sL, 1)
-    ve.wait_ge(s.sA, 1)
-    S = T.S[0:80, 0:32]
-    ve.tensor_scalar(S, T.PA[0:80, 0:32], 0.0, None, AluOpType.max).then_inc(s.sq, 1)
-    for i in range(K2):
-        ve.wait_ge(s.sq, i + 1)
-        out = S if i < K2 - 1 else T.Wd[0:80, 0:32]
-        ve.tensor_tensor(out, S, S, AluOpType.mult).then_inc(s.sq, 1)
     ve.wait_ge(s.sD, 4)
     ve.reciprocal(T.rden[0:8, 0:4], T.PD[0:8, 0:4]).then_inc(s.sR, 1)
     ve.wait_ge(s.sR, 1)
-    ve.wait_ge(s.sO1, 2)
-    for c in (0, 1):
-        ve.tensor_scalar(T.Y[0:8, c * 128:(c + 1) * 128], T.PO1[0:8, c * 128:(c + 1) * 128],
+    for c in (0, 2):
+        ve.wait_ge(SO[c], 1)
+        ve.tensor_scalar(T.Y[0:8, c * 128:(c + 1) * 128], PO[c][0:8, 0:128],
                          T.rden[0:8, c:c + 1], None, AluOpType.mult).then_inc(s.fin, 1)
+
+    S = T.S[0:80, 0:32]
+    ac.wait_ge(s.sA, 1)
+    ac.activation(S, T.PA[0:80, 0:32], AF.Relu).then_inc(s.sq, 1)
+    ac.wait_ge(s.sq, 1)
+    ac.activation(S, S, AF.Square).then_inc(s.sq, 1)
+    ac.wait_ge(s.sq, 2)
+    ac.activation(S, S, AF.Square, bias=0.5, scale=0.5).then_inc(s.sq, 1)
+    for i in range(3, NSTEP):
+        ac.wait_ge(s.sq, i)
+        out = S if i < NSTEP - 1 else T.Wd[0:80, 0:32]
+        ac.activation(out, S, AF.Square).then_inc(s.sq, 1)
     ac.wait_ge(s.sR, 1)
-    ac.wait_ge(s.sO2, 2)
-    for c in (2, 3):
-        ac.activation(T.Y[0:8, c * 128:(c + 1) * 128], T.PO2[0:8, (c - 2) * 128:(c - 1) * 128],
-                      ActivationFunctionType.Copy, scale=T.rden[0:8, c:c + 1]).then_inc(s.fin, 1)
+    for c in (1, 3):
+        ac.wait_ge(SO[c], 1)
+        ac.activation(T.Y[0:8, c * 128:(c + 1) * 128], PO[c][0:8, 0:128],
+                      AF.Copy, scale=T.rden[0:8, c:c + 1]).then_inc(s.fin, 1)
 
     sy.wait_ge(s.fin, 4)
     sy.dma_start(T.y[:, :], T.Y[0:8, :]).then_inc(s.st, 16)

@@ -2,9 +2,12 @@ from concourse.bass import DstId, RemoteDMATransfer
 from concourse.mybir import AluOpType, AxisListType, ActivationFunctionType
 
 N = 10
-K2 = 4
-INV = 1.0 / (2 ** K2)
-NSTEP = K2 + 2
+X0 = 10.528024445809836
+COEF = [[-1.2208933014692498, 3.22781902981082e-05],
+        [0.901365737391719, 0.33264135249629173],
+        [0.7644370426585919, 0.7449964286027962],
+        [0.13010170830272655, -0.0895367269222079]]
+NSTEP = len(COEF)
 
 SCRATCH = {
     "oland": ("dram", [N, 128, 32], "bfloat16"),
@@ -13,19 +16,20 @@ SCRATCH = {
     "mlT": ("sbuf", [128, 64], "float32"),
     "mlP": ("sbuf", [128, 8], "float32"),
     "lb": ("sbuf", [128, 4], "bfloat16"),
-    "cinv": ("sbuf", [128, 80], "float32"),
+    "x0b": ("sbuf", [128, 80], "float32"),
     "one1": ("sbuf", [128, 80], "float32"),
-    "Jsel": ("sbuf", [128, 80], "float32"),
-    "U": ("sbuf", [128, 80], "float32"),
+    "J1": ("sbuf", [128, 80], "float32"),
+    "Bp": ("sbuf", [128, 80], "float32"),
     "V": ("sbuf", [128, 32], "float32"),
     "I32": ("sbuf", [128, 32], "float32"),
     "negM": ("sbuf", [128, 4], "float32"),
-    "Dg": ("sbuf", [128, 32], "float32"),
+    "Lu": ("sbuf", [128, 80], "float32"),
     "S": ("sbuf", [128, 32], "float32"),
     "Wd": ("sbuf", [128, 32], "bfloat16"),
     "rden": ("sbuf", [128, 4], "float32"),
     "Y": ("sbuf", [128, 512], "bfloat16"),
     "PT": ("psum", [128, 512], "float32"),
+    "PB": ("psum", [128, 512], "float32"),
     "PA": ("psum", [128, 512], "float32"),
     "PD": ("psum", [128, 512], "float32"),
     "PO0": ("psum", [128, 512], "float32"),
@@ -33,7 +37,7 @@ SCRATCH = {
     "PO2": ("psum", [128, 512], "float32"),
     "PO3": ("psum", [128, 512], "float32"),
 }
-SEMAPHORES = ["ldm", "ldo", "mlarr", "oarr", "sent", "cst", "cg", "sT", "sP", "sX", "sT1", "sM", "sDg", "sL",
+SEMAPHORES = ["ldm", "ldo", "mlarr", "oarr", "sent", "cst", "cg", "sT", "sP", "sX", "sT1", "sB", "sM", "sLu", "sL",
               "sA", "sq", "sD", "sR", "sO0", "sO1", "sO2", "sO3", "fin", "st"]
 
 
@@ -59,7 +63,7 @@ def rank_program(g, core, T, topo):
     ac.dma_start(T.mland[r, 64:128, :], T.ml[:, :]).then_inc(s.ldm, 16)
     sy.dma_start(T.oland[r], T.o[:, :]).then_inc(s.ldo, 16)
 
-    ve.memset(T.cinv[0:32, 0:80], INV).then_inc(s.cst, 1)
+    ve.memset(T.x0b[0:8, 0:80], X0).then_inc(s.cst, 1)
     ve.memset(T.one1[0:32, 0:80], 1.0).then_inc(s.cst, 1)
 
     g.wait_ge(s.ldm, 32)
@@ -72,10 +76,10 @@ def rank_program(g, core, T, topo):
                        local_sem=s.sent)
     g.wait_ge(s.cst, 2)
     eq = AluOpType.is_equal
-    g.affine_select(T.U[0:8, 0:80], T.one1[0:8, 0:80], [[0, 10], [-1, 8]], eq, 0.0, 0, 1).then_inc(s.cg, 1)
+    g.affine_select(T.Bp[0:8, 0:80], T.x0b[0:8, 0:80], [[0, 10], [-1, 8]], eq, -1.0e4, 0, 1).then_inc(s.cg, 1)
     g.affine_select(T.V[0:8, 0:32], T.one1[0:8, 0:32], [[-1, 8], [0, 4]], eq, 0.0, 0, 1).then_inc(s.cg, 1)
     g.affine_select(T.I32[0:32, 0:32], T.one1[0:32, 0:32], [[-1, 32]], eq, 0.0, 0, 1).then_inc(s.cg, 1)
-    g.affine_select(T.Jsel[0:10, 0:80], T.cinv[0:10, 0:80], [[-1, 10], [0, 8]], eq, 0.0, 0, 1).then_inc(s.cg, 1)
+    g.affine_select(T.J1[0:10, 0:80], T.one1[0:10, 0:80], [[-1, 10], [0, 8]], eq, 0.0, 0, 1).then_inc(s.cg, 1)
     g.wait_ge(s.sent, n_ml + n_o)
 
     sy.wait_ge(s.ldm, 32)
@@ -92,12 +96,12 @@ def rank_program(g, core, T, topo):
     PO = [T.PO0, T.PO1, T.PO2, T.PO3]
     SO = [s.sO0, s.sO1, s.sO2, s.sO3]
     pe.wait_ge(s.cg, 4)
-    pe.matmul(T.PA[0:80, 0:32], T.U[0:8, 0:80], T.V[0:8, 0:32], True, False)
+    pe.matmul(T.PB[0:32, 0:80], T.V[0:8, 0:32], T.Bp[0:8, 0:80], True, False)
     pe.wait_ge(s.sT, 16)
     pe.matmul(T.PT[0:32, 0:10], mT, T.I32[0:10, 0:10], True, True).then_inc(s.sT1, 1)
-    pe.matmul(T.PA[0:80, 0:32], T.Jsel[0:10, 0:80], mT, False, False)
-    pe.wait_ge(s.sDg, 1)
-    pe.matmul(T.PA[0:80, 0:32], T.cinv[0:32, 0:80], T.Dg[0:32, 0:32], False, True).then_inc(s.sA, 1)
+    pe.matmul(T.PB[0:32, 0:80], mT, T.J1[0:10, 0:80], False, True).then_inc(s.sB, 1)
+    pe.wait_ge(s.sLu, 1)
+    pe.matmul(T.PA[0:80, 0:32], T.Lu[0:32, 0:80], T.I32[0:32, 0:32], True, True).then_inc(s.sA, 1)
     pe.wait_ge(s.sL, 1)
     pe.wait_ge(s.sq, NSTEP)
     for c in range(4):
@@ -110,9 +114,10 @@ def rank_program(g, core, T, topo):
     ve.wait_ge(s.sT1, 1)
     ve.tensor_reduce(T.negM[0:32, 0:1], T.PT[0:32, 0:10], AxisListType.X, AluOpType.max,
                      negate=True).then_inc(s.sM, 1)
-    ve.wait_ge(s.cg, 4)
+    ve.wait_ge(s.sB, 1)
     ve.wait_ge(s.sM, 1)
-    ve.tensor_scalar(T.Dg[0:32, 0:32], T.I32[0:32, 0:32], T.negM[0:32, 0:1], None, AluOpType.mult).then_inc(s.sDg, 1)
+    ve.tensor_scalar(T.Lu[0:32, 0:80], T.PB[0:32, 0:80], T.negM[0:32, 0:1], 0.0,
+                     AluOpType.add, AluOpType.max).then_inc(s.sLu, 1)
     ve.wait_ge(s.sP, 16)
     ve.tensor_copy(T.lb[0:80, 0:4], T.mlP[0:80, 1:8:2]).then_inc(s.sL, 1)
     ve.wait_ge(s.sD, 4)
@@ -125,15 +130,16 @@ def rank_program(g, core, T, topo):
 
     S = T.S[0:80, 0:32]
     ac.wait_ge(s.sA, 1)
-    ac.activation(S, T.PA[0:80, 0:32], AF.Relu).then_inc(s.sq, 1)
-    ac.wait_ge(s.sq, 1)
-    ac.activation(S, S, AF.Square).then_inc(s.sq, 1)
-    ac.wait_ge(s.sq, 2)
-    ac.activation(S, S, AF.Square, bias=0.5, scale=0.5).then_inc(s.sq, 1)
-    for i in range(3, NSTEP):
-        ac.wait_ge(s.sq, i)
+    for i in range(NSTEP):
+        a, b = COEF[i]
+        src = S
+        if i == 0:
+            src = T.PA[0:80, 0:32]
+            a = a / X0
+        else:
+            ac.wait_ge(s.sq, i)
         out = S if i < NSTEP - 1 else T.Wd[0:80, 0:32]
-        ac.activation(out, S, AF.Square).then_inc(s.sq, 1)
+        ac.activation(out, src, AF.Square, bias=b, scale=a).then_inc(s.sq, 1)
     ac.wait_ge(s.sR, 1)
     for c in (1, 3):
         ac.wait_ge(SO[c], 1)

@@ -2,43 +2,38 @@ from concourse.bass import DstId, RemoteDMATransfer
 from concourse.mybir import AluOpType, AxisListType, ActivationFunctionType
 
 N = 10
-X0 = 10.528024445809836
-COEF = [[-1.2208933014692498, 3.22781902981082e-05],
-        [0.901365737391719, 0.33264135249629173],
-        [0.7644370426585919, 0.7449964286027962],
-        [0.13010170830272655, -0.0895367269222079]]
-NSTEP = len(COEF)
+NEG = -1.0e4
 
 SCRATCH = {
     "oland": ("dram", [N, 128, 32], "bfloat16"),
     "mland": ("dram", [N, 128, 1], "float32"),
     "X": ("sbuf", [128, 512], "bfloat16"),
     "mlT": ("sbuf", [128, 64], "float32"),
-    "mlP": ("sbuf", [128, 8], "float32"),
-    "lb": ("sbuf", [128, 4], "bfloat16"),
-    "x0b": ("sbuf", [128, 80], "float32"),
+    "zer": ("sbuf", [128, 80], "float32"),
     "one1": ("sbuf", [128, 80], "float32"),
-    "J1": ("sbuf", [128, 80], "float32"),
-    "Bp": ("sbuf", [128, 80], "float32"),
+    "oneb": ("sbuf", [128, 128], "bfloat16"),
+    "Vneg": ("sbuf", [128, 32], "float32"),
     "V": ("sbuf", [128, 32], "float32"),
-    "I32": ("sbuf", [128, 32], "float32"),
+    "Bp": ("sbuf", [128, 80], "float32"),
+    "J1": ("sbuf", [128, 80], "float32"),
+    "Isel": ("sbuf", [128, 128], "bfloat16"),
     "negM": ("sbuf", [128, 4], "float32"),
-    "Lu": ("sbuf", [128, 80], "float32"),
-    "S": ("sbuf", [128, 32], "float32"),
-    "Wd": ("sbuf", [128, 32], "bfloat16"),
+    "E": ("sbuf", [128, 80], "bfloat16"),
+    "Ws": ("sbuf", [128, 128], "bfloat16"),
+    "T1": ("sbuf", [128, 80], "float32"),
+    "den": ("sbuf", [128, 4], "float32"),
     "rden": ("sbuf", [128, 4], "float32"),
-    "Y": ("sbuf", [128, 512], "bfloat16"),
+    "Y": ("sbuf", [128, 128], "bfloat16"),
     "PT": ("psum", [128, 512], "float32"),
     "PB": ("psum", [128, 512], "float32"),
-    "PA": ("psum", [128, 512], "float32"),
-    "PD": ("psum", [128, 512], "float32"),
-    "PO0": ("psum", [128, 512], "float32"),
-    "PO1": ("psum", [128, 512], "float32"),
-    "PO2": ("psum", [128, 512], "float32"),
-    "PO3": ("psum", [128, 512], "float32"),
+    "PL": ("psum", [128, 512], "float32"),
+    "PA0": ("psum", [128, 512], "float32"),
+    "PA1": ("psum", [128, 512], "float32"),
+    "POa": ("psum", [128, 512], "float32"),
+    "POb": ("psum", [128, 512], "float32"),
 }
-SEMAPHORES = ["ldm", "ldo", "mlarr", "oarr", "sent", "cst", "cg", "sT", "sP", "sX", "sT1", "sB", "sM", "sLu", "sL",
-              "sA", "sq", "sD", "sR", "sO0", "sO1", "sO2", "sO3", "fin", "st"]
+SEMAPHORES = ["ldm", "ldo", "mlarr", "oarr", "sent", "cst0", "cst1", "cgV", "sV01", "cgA", "cgI", "sT", "sX", "sT1",
+              "sB", "sPL", "sM", "sE", "sA0", "sA1", "sC0", "sC1", "sV1", "sV2", "sR", "sOa", "sOb", "fin", "st"]
 
 
 def rank_program(g, core, T, topo):
@@ -57,15 +52,20 @@ def rank_program(g, core, T, topo):
 
     sy, ac, ve, pe = g.sync, g.scalar, g.vector, g.tensor
     AF = ActivationFunctionType
+    eq = AluOpType.is_equal
     mT = T.mlT[0:10, 0:64:2]
+    lT = T.mlT[0:10, 1:64:2]
 
     sy.dma_start(T.mland[r, 0:64, :], T.ml[:, :]).then_inc(s.ldm, 16)
     ac.dma_start(T.mland[r, 64:128, :], T.ml[:, :]).then_inc(s.ldm, 16)
     sy.dma_start(T.oland[r], T.o[:, :]).then_inc(s.ldo, 16)
 
-    ve.memset(T.x0b[0:8, 0:80], X0).then_inc(s.cst, 1)
-    ve.memset(T.one1[0:32, 0:80], 1.0).then_inc(s.cst, 1)
+    ve.memset(T.zer[0:8, 0:80], 0.0).then_inc(s.cst0, 1)
+    ve.memset(T.one1[0:10, 0:80], 1.0).then_inc(s.cst1, 1)
+    ve.memset(T.oneb[0:32, 0:128], 1.0).then_inc(s.cst1, 1)
 
+    g.wait_ge(s.cst0, 1)
+    g.affine_select(T.Vneg[0:8, 0:32], T.zer[0:8, 0:32], [[-1, 8], [0, 4]], eq, NEG, 0, 1).then_inc(s.cgV, 1)
     g.wait_ge(s.ldm, 32)
     g.remote_dma_fused([RemoteDMATransfer(dst_ids=ids, dma_engine_mask=e_ml, remote_sem=s.mlarr,
                                           srcs=[T.mland[r]], dsts=[T.mland[r] for _ in others], alu_op=0)],
@@ -74,12 +74,11 @@ def rank_program(g, core, T, topo):
     g.remote_dma_fused([RemoteDMATransfer(dst_ids=ids, dma_engine_mask=e_o, remote_sem=s.oarr,
                                           srcs=[T.oland[r]], dsts=[T.oland[r] for _ in others], alu_op=0)],
                        local_sem=s.sent)
-    g.wait_ge(s.cst, 2)
-    eq = AluOpType.is_equal
-    g.affine_select(T.Bp[0:8, 0:80], T.x0b[0:8, 0:80], [[0, 10], [-1, 8]], eq, -1.0e4, 0, 1).then_inc(s.cg, 1)
-    g.affine_select(T.V[0:8, 0:32], T.one1[0:8, 0:32], [[-1, 8], [0, 4]], eq, 0.0, 0, 1).then_inc(s.cg, 1)
-    g.affine_select(T.I32[0:32, 0:32], T.one1[0:32, 0:32], [[-1, 32]], eq, 0.0, 0, 1).then_inc(s.cg, 1)
-    g.affine_select(T.J1[0:10, 0:80], T.one1[0:10, 0:80], [[-1, 10], [0, 8]], eq, 0.0, 0, 1).then_inc(s.cg, 1)
+    g.wait_ge(s.cst1, 2)
+    g.affine_select(T.Bp[0:8, 0:80], T.zer[0:8, 0:80], [[0, 10], [-1, 8]], eq, NEG, 0, 1).then_inc(s.cgA, 1)
+    g.affine_select(T.J1[0:10, 0:80], T.one1[0:10, 0:80], [[-1, 10], [0, 8]], eq, 0.0, 0, 1).then_inc(s.cgA, 1)
+    g.affine_select(T.Isel[0:32, 0:128], T.oneb[0:32, 0:128], [[64, 4], [-4, 8], [-65, 4]], eq, 0.0, 0,
+                    1).then_inc(s.cgI, 1)
     g.wait_ge(s.sent, n_ml + n_o)
 
     sy.wait_ge(s.ldm, 32)
@@ -89,63 +88,58 @@ def rank_program(g, core, T, topo):
     sy.wait_ge(s.oarr, 9 * n_o)
     sy.dma_start(T.X[0:80, :], T.oland[:]).then_inc(s.sX, 16)
 
-    ac.wait_ge(s.ldm, 32)
-    ac.wait_ge(s.mlarr, 9 * n_ml)
-    ac.dma_start(T.mlP[0:80, 0:8], T.mland[:, 0:64, :]).then_inc(s.sP, 16)
-
-    PO = [T.PO0, T.PO1, T.PO2, T.PO3]
-    SO = [s.sO0, s.sO1, s.sO2, s.sO3]
-    pe.wait_ge(s.cg, 4)
+    pe.wait_ge(s.sV01, 1)
+    pe.wait_ge(s.cgA, 2)
     pe.matmul(T.PB[0:32, 0:80], T.V[0:8, 0:32], T.Bp[0:8, 0:80], True, False)
     pe.wait_ge(s.sT, 16)
-    pe.matmul(T.PT[0:32, 0:10], mT, T.I32[0:10, 0:10], True, True).then_inc(s.sT1, 1)
+    pe.matmul(T.PT[0:32, 0:10], mT, T.J1[0:10, 0:80:8], True, True).then_inc(s.sT1, 1)
     pe.matmul(T.PB[0:32, 0:80], mT, T.J1[0:10, 0:80], False, True).then_inc(s.sB, 1)
-    pe.wait_ge(s.sLu, 1)
-    pe.matmul(T.PA[0:80, 0:32], T.Lu[0:32, 0:80], T.I32[0:32, 0:32], True, True).then_inc(s.sA, 1)
-    pe.wait_ge(s.sL, 1)
-    pe.wait_ge(s.sq, NSTEP)
-    for c in range(4):
-        pe.matmul(T.PD[0:8, c:c + 1], T.Wd[0:80, c:32:4], T.lb[0:80, c:c + 1], True, True).then_inc(s.sD, 1)
+    pe.matmul(T.PL[0:32, 0:80], lT, T.J1[0:10, 0:80], True, True).then_inc(s.sPL, 1)
+    pe.wait_ge(s.cgI, 1)
+    pe.wait_ge(s.sE, 1)
+    pe.matmul(T.PA0[0:80, 0:64], T.E[0:32, 0:80], T.Isel[0:32, 0:64], True, True).then_inc(s.sA0, 1)
+    pe.matmul(T.PA1[0:80, 0:64], T.E[0:32, 0:80], T.Isel[0:32, 64:128], True, True).then_inc(s.sA1, 1)
+    PO = [T.POa, T.POb]
+    SO = [s.sOa, s.sOb]
     pe.wait_ge(s.sX, 16)
-    for c in range(4):
-        pe.matmul(PO[c][0:8, 0:128], T.Wd[0:80, c:32:4], T.X[0:80, c * 128:(c + 1) * 128],
-                  True, True).then_inc(SO[c], 1)
+    pe.wait_ge(s.sC0, 1)
+    for a in range(2):
+        for c in (0, 1):
+            pe.matmul(PO[a][0:32, 0:64], T.Ws[0:80, c * 32:(c + 1) * 32],
+                      T.X[0:80, c * 128 + a * 64:c * 128 + a * 64 + 64], c == 0, False)
+    pe.wait_ge(s.sC1, 1)
+    for a in range(2):
+        pe.matmul(PO[a][0:32, 0:64], T.Ws[0:80, 64:96], T.X[0:80, 256 + a * 64:256 + a * 64 + 64], False, False)
+        pe.matmul(PO[a][0:32, 0:64], T.Ws[0:80, 96:128], T.X[0:80, 384 + a * 64:384 + a * 64 + 64],
+                  False, True).then_inc(SO[a], 1)
 
     ve.wait_ge(s.sT1, 1)
     ve.tensor_reduce(T.negM[0:32, 0:1], T.PT[0:32, 0:10], AxisListType.X, AluOpType.max,
                      negate=True).then_inc(s.sM, 1)
-    ve.wait_ge(s.sB, 1)
-    ve.wait_ge(s.sM, 1)
-    ve.tensor_scalar(T.Lu[0:32, 0:80], T.PB[0:32, 0:80], T.negM[0:32, 0:1], 0.0,
-                     AluOpType.add, AluOpType.max).then_inc(s.sLu, 1)
-    ve.wait_ge(s.sP, 16)
-    ve.tensor_copy(T.lb[0:80, 0:4], T.mlP[0:80, 1:8:2]).then_inc(s.sL, 1)
-    ve.wait_ge(s.sD, 4)
-    ve.reciprocal(T.rden[0:8, 0:4], T.PD[0:8, 0:4]).then_inc(s.sR, 1)
+    ve.wait_ge(s.sPL, 1)
+    ve.wait_ge(s.sE, 1)
+    ve.tensor_tensor(T.T1[0:32, 0:80], T.E[0:32, 0:80], T.PL[0:32, 0:80], AluOpType.mult).then_inc(s.sV1, 1)
+    ve.wait_ge(s.sV1, 1)
+    ve.tensor_reduce(T.den[0:32, 0:1], T.T1[0:32, 0:80], AxisListType.X, AluOpType.add).then_inc(s.sV2, 1)
+    ve.wait_ge(s.sV2, 1)
+    ve.reciprocal(T.rden[0:32, 0:1], T.den[0:32, 0:1]).then_inc(s.sR, 1)
     ve.wait_ge(s.sR, 1)
-    for c in (0, 2):
-        ve.wait_ge(SO[c], 1)
-        ve.tensor_scalar(T.Y[0:8, c * 128:(c + 1) * 128], PO[c][0:8, 0:128],
-                         T.rden[0:8, c:c + 1], None, AluOpType.mult).then_inc(s.fin, 1)
+    ve.wait_ge(s.sOa, 1)
+    ve.tensor_scalar(T.Y[0:32, 0:64], T.POa[0:32, 0:64], T.rden[0:32, 0:1], None, AluOpType.mult).then_inc(s.fin, 1)
 
-    S = T.S[0:80, 0:32]
-    ac.wait_ge(s.sA, 1)
-    for i in range(NSTEP):
-        a, b = COEF[i]
-        src = S
-        if i == 0:
-            src = T.PA[0:80, 0:32]
-            a = a / X0
-        else:
-            ac.wait_ge(s.sq, i)
-        out = S if i < NSTEP - 1 else T.Wd[0:80, 0:32]
-        ac.activation(out, src, AF.Square, bias=b, scale=a).then_inc(s.sq, 1)
+    ac.wait_ge(s.cgV, 1)
+    ac.activation(T.V[0:8, 0:32], T.Vneg[0:8, 0:32], AF.Exp).then_inc(s.sV01, 1)
+    ac.wait_ge(s.sB, 1)
+    ac.wait_ge(s.sM, 1)
+    ac.activation(T.E[0:32, 0:80], T.PB[0:32, 0:80], AF.Exp, bias=T.negM[0:32, 0:1]).then_inc(s.sE, 1)
+    ac.wait_ge(s.sA0, 1)
+    ac.activation(T.Ws[0:80, 0:64], T.PA0[0:80, 0:64], AF.Copy).then_inc(s.sC0, 1)
+    ac.wait_ge(s.sA1, 1)
+    ac.activation(T.Ws[0:80, 64:128], T.PA1[0:80, 0:64], AF.Copy).then_inc(s.sC1, 1)
     ac.wait_ge(s.sR, 1)
-    for c in (1, 3):
-        ac.wait_ge(SO[c], 1)
-        ac.activation(T.Y[0:8, c * 128:(c + 1) * 128], PO[c][0:8, 0:128],
-                      AF.Copy, scale=T.rden[0:8, c:c + 1]).then_inc(s.fin, 1)
+    ac.wait_ge(s.sOb, 1)
+    ac.activation(T.Y[0:32, 64:128], T.POb[0:32, 0:64], AF.Copy, scale=T.rden[0:32, 0:1]).then_inc(s.fin, 1)
 
-    sy.wait_ge(s.fin, 4)
-    sy.dma_start(T.y[:, :], T.Y[0:8, :]).then_inc(s.st, 16)
+    sy.wait_ge(s.fin, 2)
+    sy.dma_start(T.y[:, :], T.Y[0:32, 0:128]).then_inc(s.st, 16)
     sy.wait_ge(s.st, 16)

@@ -7,33 +7,30 @@ NEG = -1.0e4
 SCRATCH = {
     "oland": ("dram", [N, 128, 32], "bfloat16"),
     "mland": ("dram", [N, 128, 1], "float32"),
-    "X": ("sbuf", [128, 512], "bfloat16"),
-    "mlT": ("sbuf", [128, 64], "float32"),
-    "zer": ("sbuf", [128, 80], "float32"),
-    "one1": ("sbuf", [128, 80], "float32"),
-    "oneb": ("sbuf", [128, 128], "bfloat16"),
-    "Vneg": ("sbuf", [128, 32], "float32"),
-    "V": ("sbuf", [128, 32], "float32"),
-    "Bp": ("sbuf", [128, 80], "float32"),
-    "J1": ("sbuf", [128, 80], "float32"),
-    "Isel": ("sbuf", [128, 128], "bfloat16"),
+    "X2": ("sbuf", [128, 384], "bfloat16"),
+    "mTile": ("sbuf", [128, 256], "float32"),
+    "mBlk": ("sbuf", [128, 256], "float32"),
+    "zer": ("sbuf", [128, 128], "float32"),
+    "one1": ("sbuf", [128, 96], "float32"),
+    "Aneg": ("sbuf", [128, 128], "float32"),
+    "L2": ("sbuf", [128, 128], "float32"),
+    "R": ("sbuf", [128, 96], "float32"),
+    "I10": ("sbuf", [128, 12], "float32"),
     "negM": ("sbuf", [128, 4], "float32"),
-    "E": ("sbuf", [128, 80], "bfloat16"),
-    "Ws": ("sbuf", [128, 128], "bfloat16"),
-    "T1": ("sbuf", [128, 80], "float32"),
-    "den": ("sbuf", [128, 4], "float32"),
+    "Wd": ("sbuf", [128, 96], "bfloat16"),
+    "lcol": ("sbuf", [128, 8], "bfloat16"),
     "rden": ("sbuf", [128, 4], "float32"),
     "Y": ("sbuf", [128, 128], "bfloat16"),
-    "PT": ("psum", [128, 512], "float32"),
-    "PB": ("psum", [128, 512], "float32"),
-    "PL": ("psum", [128, 512], "float32"),
-    "PA0": ("psum", [128, 512], "float32"),
-    "PA1": ("psum", [128, 512], "float32"),
+    "PT5": ("psum", [128, 512], "float32"),
+    "ARG": ("psum", [128, 512], "float32"),
+    "PLC": ("psum", [128, 512], "float32"),
+    "PD": ("psum", [128, 512], "float32"),
     "POa": ("psum", [128, 512], "float32"),
     "POb": ("psum", [128, 512], "float32"),
 }
-SEMAPHORES = ["ldm", "ldo", "mlarr", "oarr", "sent", "cst0", "cst1", "cgV", "sV01", "cgA", "cgI", "sT", "sX", "sT1",
-              "sB", "sPL", "sM", "sE", "sA0", "sA1", "sC0", "sC1", "sV1", "sV2", "sR", "sOa", "sOb", "fin", "st"]
+SEMAPHORES = ["ldm", "ldo", "mlarr", "sent", "cst0", "cst1", "cstB", "cgV", "sL2", "cgR", "cgA", "sT", "sK",
+              "sX0", "sX1", "sX2", "sT1", "sB", "sPL", "sLC", "sM", "sE01", "sE2", "sD", "sR", "sOa", "sOb",
+              "fin", "st"] + ["oa%d" % j for j in range(N)]
 
 
 def rank_program(g, core, T, topo):
@@ -41,7 +38,7 @@ def rank_program(g, core, T, topo):
     if r is None:
         return
     s = T.sem
-    others = [c for c in T.cores if c != core]
+    others = [T.cores[(r + k) % N] for k in range(1, N)]
     common = 0xFFFF
     for c in others:
         common &= topo.mask(core, c)
@@ -52,90 +49,98 @@ def rank_program(g, core, T, topo):
 
     sy, ac, ve, pe = g.sync, g.scalar, g.vector, g.tensor
     AF = ActivationFunctionType
-    eq = AluOpType.is_equal
-    mT = T.mlT[0:10, 0:64:2]
-    lT = T.mlT[0:10, 1:64:2]
+    eq, ge = AluOpType.is_equal, AluOpType.is_ge
 
-    sy.dma_start(T.mland[r, 0:64, :], T.ml[:, :]).then_inc(s.ldm, 16)
-    ac.dma_start(T.mland[r, 64:128, :], T.ml[:, :]).then_inc(s.ldm, 16)
-    sy.dma_start(T.oland[r], T.o[:, :]).then_inc(s.ldo, 16)
+    sy.dma_start(T.mland[0, 0:64, :], T.ml[:, :]).then_inc(s.ldm, 16)
+    ac.dma_start(T.mland[0, 64:128, :], T.ml[:, :]).then_inc(s.ldm, 16)
+    sy.dma_start(T.oland[0], T.o[:, :]).then_inc(s.ldo, 16)
 
-    ve.memset(T.zer[0:8, 0:80], 0.0).then_inc(s.cst0, 1)
-    ve.memset(T.one1[0:10, 0:80], 1.0).then_inc(s.cst1, 1)
-    ve.memset(T.oneb[0:32, 0:128], 1.0).then_inc(s.cst1, 1)
+    ve.memset(T.zer[0:32, 0:128], 0.0).then_inc(s.cst0, 1)
+    ve.memset(T.mBlk[0:10, 0:256], 0.0).then_inc(s.cstB, 1)
+    ve.memset(T.one1[0:10, 0:96], 1.0).then_inc(s.cst1, 1)
 
     g.wait_ge(s.cst0, 1)
-    g.affine_select(T.Vneg[0:8, 0:32], T.zer[0:8, 0:32], [[-1, 8], [0, 4]], eq, NEG, 0, 1).then_inc(s.cgV, 1)
+    g.affine_select(T.Aneg[0:32, 0:128], T.zer[0:32, 0:128], [[0, 4], [-1, 32]], eq, NEG, 0, 1).then_inc(s.cgV, 1)
     g.wait_ge(s.ldm, 32)
     g.remote_dma_fused([RemoteDMATransfer(dst_ids=ids, dma_engine_mask=e_ml, remote_sem=s.mlarr,
-                                          srcs=[T.mland[r]], dsts=[T.mland[r] for _ in others], alu_op=0)],
+                                          srcs=[T.mland[0]], dsts=[T.mland[k] for k in range(1, N)], alu_op=0)],
                        local_sem=s.sent)
     g.wait_ge(s.ldo, 16)
-    g.remote_dma_fused([RemoteDMATransfer(dst_ids=ids, dma_engine_mask=e_o, remote_sem=s.oarr,
-                                          srcs=[T.oland[r]], dsts=[T.oland[r] for _ in others], alu_op=0)],
+    g.remote_dma_fused([RemoteDMATransfer(dst_ids=ids, dma_engine_mask=e_o, remote_sem=s["oa%d" % r],
+                                          srcs=[T.oland[0]], dsts=[T.oland[k] for k in range(1, N)], alu_op=0)],
                        local_sem=s.sent)
-    g.wait_ge(s.cst1, 2)
-    g.affine_select(T.Bp[0:8, 0:80], T.zer[0:8, 0:80], [[0, 10], [-1, 8]], eq, NEG, 0, 1).then_inc(s.cgA, 1)
-    g.affine_select(T.J1[0:10, 0:80], T.one1[0:10, 0:80], [[-1, 10], [0, 8]], eq, 0.0, 0, 1).then_inc(s.cgA, 1)
-    g.affine_select(T.Isel[0:32, 0:128], T.oneb[0:32, 0:128], [[64, 4], [-4, 8], [-65, 4]], eq, 0.0, 0,
-                    1).then_inc(s.cgI, 1)
+    g.wait_ge(s.cst1, 1)
+    g.affine_select(T.I10[0:10, 0:10], T.one1[0:10, 0:10], [[-1, 10]], eq, 0.0, 0, 1).then_inc(s.cgA, 1)
+    g.affine_select(T.R[0:10, 0:96], T.one1[0:10, 0:96], [[-4, 3], [0, 32]], ge, 0.0, 0, 1).then_inc(s.cgR, 1)
+    g.wait_ge(s.cgR, 1)
+    g.affine_select(T.R[0:10, 0:96], T.R[0:10, 0:96], [[4, 3], [0, 32]], ge, 0.0, 3, -1).then_inc(s.cgA, 1)
     g.wait_ge(s.sent, n_ml + n_o)
 
-    sy.wait_ge(s.ldm, 32)
-    sy.wait_ge(s.mlarr, 9 * n_ml)
-    sy.dma_start(T.mlT[0:10, 0:64], T.mland[:, 0:64, :]).then_inc(s.sT, 16)
-    sy.wait_ge(s.ldo, 16)
-    sy.wait_ge(s.oarr, 9 * n_o)
-    sy.dma_start(T.X[0:80, :], T.oland[:]).then_inc(s.sX, 16)
+    def blk(q, a):
+        q.dma_start(T.mBlk[a:N:4, a * 64:(a + 1) * 64], T.mland[a:N:4, 0:64, :]).then_inc(s.sK, 16)
 
-    pe.wait_ge(s.sV01, 1)
+    for q in (sy, ac):
+        if q is ac:
+            ac.wait_ge(s.cgV, 1)
+            ac.activation(T.L2[0:32, 0:128], T.Aneg[0:32, 0:128], AF.Exp).then_inc(s.sL2, 1)
+        q.wait_ge(s.cstB, 1)
+        q.wait_ge(s.ldm, 32)
+        q.wait_ge(s.mlarr, 9 * n_ml)
+    sy.dma_start(T.mTile[0:10, 0:128], T.mland[:, :, :]).then_inc(s.sT, 16)
+    ac.dma_start(T.mTile[0:10, 128:256], T.mland[:, :, :]).then_inc(s.sT, 16)
+    blk(sy, 0)
+    blk(ac, 1)
+    blk(sy, 2)
+    blk(ac, 3)
+    SX = [s.sX0, s.sX1, s.sX2]
+    KP = [128, 128, 64]
+    sy.wait_ge(s.ldo, 16)
+    for b in range(3):
+        for k in range(4 * b, min(4 * b + 4, N)):
+            if k > 0:
+                sy.wait_ge(s["oa%d" % ((r - k) % N)], n_o)
+        sy.dma_start(T.X2[0:KP[b], b * 128:(b + 1) * 128], T.oland[4 * b:min(4 * b + 4, N)]).then_inc(SX[b], 16)
+
+    pe.wait_ge(s.cgV, 1)
+    pe.wait_ge(s.sL2, 1)
+    pe.matmul(T.ARG[0:128, 0:96], T.L2[0:32, 0:128], T.Aneg[0:32, 0:96], True, False)
     pe.wait_ge(s.cgA, 2)
-    pe.matmul(T.PB[0:32, 0:80], T.V[0:8, 0:32], T.Bp[0:8, 0:80], True, False)
-    pe.wait_ge(s.sT, 16)
-    pe.matmul(T.PT[0:32, 0:10], mT, T.J1[0:10, 0:80:8], True, True).then_inc(s.sT1, 1)
-    pe.matmul(T.PB[0:32, 0:80], mT, T.J1[0:10, 0:80], False, True).then_inc(s.sB, 1)
-    pe.matmul(T.PL[0:32, 0:80], lT, T.J1[0:10, 0:80], True, True).then_inc(s.sPL, 1)
-    pe.wait_ge(s.cgI, 1)
-    pe.wait_ge(s.sE, 1)
-    pe.matmul(T.PA0[0:80, 0:64], T.E[0:32, 0:80], T.Isel[0:32, 0:64], True, True).then_inc(s.sA0, 1)
-    pe.matmul(T.PA1[0:80, 0:64], T.E[0:32, 0:80], T.Isel[0:32, 64:128], True, True).then_inc(s.sA1, 1)
+    pe.wait_ge(s.sT, 32)
+    pe.matmul(T.PT5[0:128, 0:10], T.mTile[0:10, 0:256:2], T.I10[0:10, 0:10], True, True).then_inc(s.sT1, 1)
+    pe.wait_ge(s.sK, 64)
+    pe.matmul(T.ARG[0:128, 0:96], T.mBlk[0:10, 0:256:2], T.R[0:10, 0:96], False, True).then_inc(s.sB, 1)
+    pe.matmul(T.PLC[0:128, 0:3], T.mBlk[0:10, 1:256:2], T.R[0:10, 0:96:32], True, True).then_inc(s.sPL, 1)
+    pe.wait_ge(s.sLC, 1)
+    pe.wait_ge(s.sE01, 1)
+    for b in range(2):
+        pe.matmul(T.PD[0:32, 0:1], T.Wd[0:128, 32 * b:32 * b + 32], T.lcol[0:128, b:b + 1], b == 0, False)
+    pe.wait_ge(s.sE2, 1)
+    pe.matmul(T.PD[0:32, 0:1], T.Wd[0:64, 64:96], T.lcol[0:64, 2:3], False, True).then_inc(s.sD, 1)
     PO = [T.POa, T.POb]
     SO = [s.sOa, s.sOb]
-    pe.wait_ge(s.sX, 16)
-    pe.wait_ge(s.sC0, 1)
-    for a in range(2):
-        for c in (0, 1):
-            pe.matmul(PO[a][0:32, 0:64], T.Ws[0:80, c * 32:(c + 1) * 32],
-                      T.X[0:80, c * 128 + a * 64:c * 128 + a * 64 + 64], c == 0, False)
-    pe.wait_ge(s.sC1, 1)
-    for a in range(2):
-        pe.matmul(PO[a][0:32, 0:64], T.Ws[0:80, 64:96], T.X[0:80, 256 + a * 64:256 + a * 64 + 64], False, False)
-        pe.matmul(PO[a][0:32, 0:64], T.Ws[0:80, 96:128], T.X[0:80, 384 + a * 64:384 + a * 64 + 64],
-                  False, True).then_inc(SO[a], 1)
+    for b in range(3):
+        pe.wait_ge(SX[b], 16)
+        for h in range(2):
+            mm = pe.matmul(PO[h][0:32, 0:64], T.Wd[0:KP[b], 32 * b:32 * b + 32],
+                           T.X2[0:KP[b], b * 128 + h * 64:b * 128 + h * 64 + 64], b == 0, b == 2)
+            if b == 2:
+                mm.then_inc(SO[h], 1)
 
     ve.wait_ge(s.sT1, 1)
-    ve.tensor_reduce(T.negM[0:32, 0:1], T.PT[0:32, 0:10], AxisListType.X, AluOpType.max,
+    ve.tensor_reduce(T.negM[0:128, 0:1], T.PT5[0:128, 0:10], AxisListType.X, AluOpType.max,
                      negate=True).then_inc(s.sM, 1)
     ve.wait_ge(s.sPL, 1)
-    ve.wait_ge(s.sE, 1)
-    ve.tensor_tensor(T.T1[0:32, 0:80], T.E[0:32, 0:80], T.PL[0:32, 0:80], AluOpType.mult).then_inc(s.sV1, 1)
-    ve.wait_ge(s.sV1, 1)
-    ve.tensor_reduce(T.den[0:32, 0:1], T.T1[0:32, 0:80], AxisListType.X, AluOpType.add).then_inc(s.sV2, 1)
-    ve.wait_ge(s.sV2, 1)
-    ve.reciprocal(T.rden[0:32, 0:1], T.den[0:32, 0:1]).then_inc(s.sR, 1)
+    ve.tensor_copy(T.lcol[0:128, 0:3], T.PLC[0:128, 0:3]).then_inc(s.sLC, 1)
+    ve.wait_ge(s.sD, 1)
+    ve.reciprocal(T.rden[0:32, 0:1], T.PD[0:32, 0:1]).then_inc(s.sR, 1)
     ve.wait_ge(s.sR, 1)
     ve.wait_ge(s.sOa, 1)
     ve.tensor_scalar(T.Y[0:32, 0:64], T.POa[0:32, 0:64], T.rden[0:32, 0:1], None, AluOpType.mult).then_inc(s.fin, 1)
 
-    ac.wait_ge(s.cgV, 1)
-    ac.activation(T.V[0:8, 0:32], T.Vneg[0:8, 0:32], AF.Exp).then_inc(s.sV01, 1)
     ac.wait_ge(s.sB, 1)
     ac.wait_ge(s.sM, 1)
-    ac.activation(T.E[0:32, 0:80], T.PB[0:32, 0:80], AF.Exp, bias=T.negM[0:32, 0:1]).then_inc(s.sE, 1)
-    ac.wait_ge(s.sA0, 1)
-    ac.activation(T.Ws[0:80, 0:64], T.PA0[0:80, 0:64], AF.Copy).then_inc(s.sC0, 1)
-    ac.wait_ge(s.sA1, 1)
-    ac.activation(T.Ws[0:80, 64:128], T.PA1[0:80, 0:64], AF.Copy).then_inc(s.sC1, 1)
+    ac.activation(T.Wd[0:128, 0:64], T.ARG[0:128, 0:64], AF.Exp, bias=T.negM[0:128, 0:1]).then_inc(s.sE01, 1)
+    ac.activation(T.Wd[0:64, 64:96], T.ARG[0:64, 64:96], AF.Exp, bias=T.negM[0:64, 0:1]).then_inc(s.sE2, 1)
     ac.wait_ge(s.sR, 1)
     ac.wait_ge(s.sOb, 1)
     ac.activation(T.Y[0:32, 64:128], T.POb[0:32, 0:64], AF.Copy, scale=T.rden[0:32, 0:1]).then_inc(s.fin, 1)

from concourse.bass import DstId, RemoteDMATransfer
from concourse.mybir import AluOpType, AxisListType, ActivationFunctionType

N = 10
NEG = -1.0e4

SCRATCH = {
    "oland": ("dram", [N, 128, 32], "bfloat16"),
    "mland": ("dram", [N, 128, 1], "float32"),
    "X2": ("sbuf", [128, 384], "bfloat16"),
    "mTile": ("sbuf", [128, 256], "float32"),
    "mBlk": ("sbuf", [128, 256], "float32"),
    "zer": ("sbuf", [128, 128], "float32"),
    "one1": ("sbuf", [128, 96], "float32"),
    "Aneg": ("sbuf", [128, 128], "float32"),
    "L2": ("sbuf", [128, 128], "float32"),
    "R": ("sbuf", [128, 96], "float32"),
    "I10": ("sbuf", [128, 12], "float32"),
    "negM": ("sbuf", [128, 4], "float32"),
    "Wd": ("sbuf", [128, 96], "bfloat16"),
    "lcol": ("sbuf", [128, 8], "bfloat16"),
    "rden": ("sbuf", [128, 4], "float32"),
    "Y": ("sbuf", [128, 128], "bfloat16"),
    "PT5": ("psum", [128, 512], "float32"),
    "ARG": ("psum", [128, 512], "float32"),
    "PLC": ("psum", [128, 512], "float32"),
    "PD": ("psum", [128, 512], "float32"),
    "POa": ("psum", [128, 512], "float32"),
    "POb": ("psum", [128, 512], "float32"),
}
SEMAPHORES = ["ldm", "ldo", "mlarr", "sent", "cst0", "cst1", "cstB", "cgV", "sL2", "cgR", "cgA", "sT", "sK",
              "sX0", "sX1", "sX2", "sT1", "sB", "sPL", "sLC", "sM", "sE01", "sE2", "sD", "sR", "sOa", "sOb",
              "fin", "st"] + ["oa%d" % j for j in range(N)]


def rank_program(g, core, T, topo):
    r = T.rank_of(core)
    if r is None:
        return
    s = T.sem
    others = [T.cores[(r + k) % N] for k in range(1, N)]
    common = 0xFFFF
    for c in others:
        common &= topo.mask(core, c)
    bits = [1 << b for b in range(16) if (common >> b) & 1]
    ids = [DstId(rid=topo.addr(c)[0], pnc=topo.addr(c)[1]) for c in others]
    e_ml, n_ml = bits[0], 1
    e_o, n_o = common, len(bits)

    sy, ac, ve, pe = g.sync, g.scalar, g.vector, g.tensor
    AF = ActivationFunctionType
    eq, ge = AluOpType.is_equal, AluOpType.is_ge

    sy.dma_start(T.mland[0, 0:64, :], T.ml[:, :]).then_inc(s.ldm, 16)
    ac.dma_start(T.mland[0, 64:128, :], T.ml[:, :]).then_inc(s.ldm, 16)
    sy.dma_start(T.oland[0], T.o[:, :]).then_inc(s.ldo, 16)

    ve.memset(T.zer[0:32, 0:128], 0.0).then_inc(s.cst0, 1)
    ve.memset(T.mBlk[0:10, 0:256], 0.0).then_inc(s.cstB, 1)
    ve.memset(T.one1[0:10, 0:96], 1.0).then_inc(s.cst1, 1)

    g.wait_ge(s.cst0, 1)
    g.affine_select(T.Aneg[0:32, 0:128], T.zer[0:32, 0:128], [[0, 4], [-1, 32]], eq, NEG, 0, 1).then_inc(s.cgV, 1)
    g.wait_ge(s.ldm, 32)
    g.remote_dma_fused([RemoteDMATransfer(dst_ids=ids, dma_engine_mask=e_ml, remote_sem=s.mlarr,
                                          srcs=[T.mland[0]], dsts=[T.mland[k] for k in range(1, N)], alu_op=0)],
                       local_sem=s.sent)
    g.wait_ge(s.ldo, 16)
    g.remote_dma_fused([RemoteDMATransfer(dst_ids=ids, dma_engine_mask=e_o, remote_sem=s["oa%d" % r],
                                          srcs=[T.oland[0]], dsts=[T.oland[k] for k in range(1, N)], alu_op=0)],
                       local_sem=s.sent)
    g.wait_ge(s.cst1, 1)
    g.affine_select(T.I10[0:10, 0:10], T.one1[0:10, 0:10], [[-1, 10]], eq, 0.0, 0, 1).then_inc(s.cgA, 1)
    g.affine_select(T.R[0:10, 0:96], T.one1[0:10, 0:96], [[-4, 3], [0, 32]], ge, 0.0, 0, 1).then_inc(s.cgR, 1)
    g.wait_ge(s.cgR, 1)
    g.affine_select(T.R[0:10, 0:96], T.R[0:10, 0:96], [[4, 3], [0, 32]], ge, 0.0, 3, -1).then_inc(s.cgA, 1)
    g.wait_ge(s.sent, n_ml + n_o)

    def blk(q, a):
        q.dma_start(T.mBlk[a:N:4, a * 64:(a + 1) * 64], T.mland[a:N:4, 0:64, :]).then_inc(s.sK, 16)

    for q in (sy, ac):
        if q is ac:
            ac.wait_ge(s.cgV, 1)
            ac.activation(T.L2[0:32, 0:128], T.Aneg[0:32, 0:128], AF.Exp).then_inc(s.sL2, 1)
        q.wait_ge(s.cstB, 1)
        q.wait_ge(s.ldm, 32)
        q.wait_ge(s.mlarr, 9 * n_ml)
    sy.dma_start(T.mTile[0:10, 0:128], T.mland[:, :, :]).then_inc(s.sT, 16)
    ac.dma_start(T.mTile[0:10, 128:256], T.mland[:, :, :]).then_inc(s.sT, 16)
    blk(sy, 0)
    blk(ac, 1)
    blk(sy, 2)
    blk(ac, 3)
    SX = [s.sX0, s.sX1, s.sX2]
    KP = [128, 128, 64]
    sy.wait_ge(s.ldo, 16)
    for b in range(3):
        for k in range(4 * b, min(4 * b + 4, N)):
            if k > 0:
                sy.wait_ge(s["oa%d" % ((r - k) % N)], n_o)
        sy.dma_start(T.X2[0:KP[b], b * 128:(b + 1) * 128], T.oland[4 * b:min(4 * b + 4, N)]).then_inc(SX[b], 16)

    pe.wait_ge(s.cgV, 1)
    pe.wait_ge(s.sL2, 1)
    pe.matmul(T.ARG[0:128, 0:96], T.L2[0:32, 0:128], T.Aneg[0:32, 0:96], True, False)
    pe.wait_ge(s.cgA, 2)
    pe.wait_ge(s.sT, 32)
    pe.matmul(T.PT5[0:128, 0:10], T.mTile[0:10, 0:256:2], T.I10[0:10, 0:10], True, True).then_inc(s.sT1, 1)
    pe.wait_ge(s.sK, 64)
    pe.matmul(T.ARG[0:128, 0:96], T.mBlk[0:10, 0:256:2], T.R[0:10, 0:96], False, True).then_inc(s.sB, 1)
    pe.matmul(T.PLC[0:128, 0:3], T.mBlk[0:10, 1:256:2], T.R[0:10, 0:96:32], True, True).then_inc(s.sPL, 1)
    pe.wait_ge(s.sLC, 1)
    pe.wait_ge(s.sE01, 1)
    for b in range(2):
        pe.matmul(T.PD[0:32, 0:1], T.Wd[0:128, 32 * b:32 * b + 32], T.lcol[0:128, b:b + 1], b == 0, False)
    pe.wait_ge(s.sE2, 1)
    pe.matmul(T.PD[0:32, 0:1], T.Wd[0:64, 64:96], T.lcol[0:64, 2:3], False, True).then_inc(s.sD, 1)
    PO = [T.POa, T.POb]
    SO = [s.sOa, s.sOb]
    for b in range(3):
        pe.wait_ge(SX[b], 16)
        for h in range(2):
            mm = pe.matmul(PO[h][0:32, 0:64], T.Wd[0:KP[b], 32 * b:32 * b + 32],
                           T.X2[0:KP[b], b * 128 + h * 64:b * 128 + h * 64 + 64], b == 0, b == 2)
            if b == 2:
                mm.then_inc(SO[h], 1)

    ve.wait_ge(s.sT1, 1)
    ve.tensor_reduce(T.negM[0:128, 0:1], T.PT5[0:128, 0:10], AxisListType.X, AluOpType.max,
                     negate=True).then_inc(s.sM, 1)
    ve.wait_ge(s.sPL, 1)
    ve.tensor_copy(T.lcol[0:128, 0:3], T.PLC[0:128, 0:3]).then_inc(s.sLC, 1)
    ve.wait_ge(s.sD, 1)
    ve.reciprocal(T.rden[0:32, 0:1], T.PD[0:32, 0:1]).then_inc(s.sR, 1)
    ve.wait_ge(s.sR, 1)
    ve.wait_ge(s.sOa, 1)
    ve.tensor_scalar(T.Y[0:32, 0:64], T.POa[0:32, 0:64], T.rden[0:32, 0:1], None, AluOpType.mult).then_inc(s.fin, 1)

    ac.wait_ge(s.sB, 1)
    ac.wait_ge(s.sM, 1)
    ac.activation(T.Wd[0:128, 0:64], T.ARG[0:128, 0:64], AF.Exp, bias=T.negM[0:128, 0:1]).then_inc(s.sE01, 1)
    ac.activation(T.Wd[0:64, 64:96], T.ARG[0:64, 64:96], AF.Exp, bias=T.negM[0:64, 0:1]).then_inc(s.sE2, 1)
    ac.wait_ge(s.sR, 1)
    ac.wait_ge(s.sOb, 1)
    ac.activation(T.Y[0:32, 64:128], T.POb[0:32, 0:64], AF.Copy, scale=T.rden[0:32, 0:1]).then_inc(s.fin, 1)

    sy.wait_ge(s.fin, 2)
    sy.dma_start(T.y[:, :], T.Y[0:32, 0:128]).then_inc(s.st, 16)
    sy.wait_ge(s.st, 16)
